import numpy as np
import ml_dtypes


def mxq(x, axis, fmt="e4m3"):
    dtype, down = {"e4m3": (ml_dtypes.float8_e4m3fn, 7), "e5m2": (ml_dtypes.float8_e5m2, 14)}[fmt]
    v = np.moveaxis(np.asarray(x, np.float32).astype(ml_dtypes.bfloat16).astype(np.float64), axis, -1)
    blocks = v.reshape(v.shape[:-1] + (-1, 32))
    amax = np.abs(blocks).max(-1, keepdims=True)
    byte = np.maximum(np.where(amax > 0, np.frexp(amax)[1] - 1 + 127, 0) - down, 1)
    scale = np.exp2(byte - 127.0)
    codes = (blocks / scale).astype(np.float32).astype(dtype).astype(np.float64)
    return np.moveaxis((codes * scale).reshape(v.shape), -1, axis)


WIDE = False


def mx_kscale(k):
    if not WIDE:
        return np.ones(k)
    levels = np.array([30, -30])
    if k % 512:
        return np.exp2(np.random.permutation(np.resize(levels, k // 32))).repeat(32)
    a = np.empty((k // 512, 16))
    for p in range(k // 512):
        a[p, :8] = np.random.permutation(np.resize(levels, 8))
        for g in range(8):
            far = levels[np.abs(levels - a[p, g]) >= 10]
            a[p, g + 8] = far[np.random.randint(len(far))]
    return np.exp2(a.ravel()).repeat(32)


def f64(x):
    return np.asarray(x).astype(np.float64)


def striped(idx):
    return np.tile(np.asarray(idx).reshape(-1, 16).T, (8, 1)).astype(np.uint16)


def unstriped(offs):
    return offs[:16].T.reshape(-1).astype(np.int64)


E2M1 = np.array([0.0, 0.5, 1.0, 1.5, 2.0, 3.0, 4.0, 6.0, -0.0, -0.5, -1.0, -1.5, -2.0, -3.0, -4.0, -6.0])


def pack_weight(w, fmt):
    k, n = w.shape
    w = f64(np.asarray(w, np.float32).astype(ml_dtypes.bfloat16)).reshape(k // 32, 32, n)
    amax = np.abs(w).max(1)
    if fmt in ("e4m3", "e5m2"):
        byte = np.frexp(amax)[1] - 1 + 127 - (7 if fmt == "e4m3" else 14)
    else:
        mant, ex = np.frexp(amax / 6.0)
        byte = np.where(mant > 0.5, ex, ex - 1) + 127
    byte = np.clip(np.where(amax > 0, byte, 1), 1, 254)
    scaled = (w * np.exp2(127.0 - byte)[:, None, :]).reshape(k, n).astype(np.float32)
    by_word = np.ascontiguousarray(scaled.reshape(k // 512, 128, 4, n).transpose(0, 1, 3, 2))
    if fmt in ("e4m3", "e5m2"):
        words = by_word.astype(ml_dtypes.float8_e4m3fn if fmt == "e4m3" else ml_dtypes.float8_e5m2).view(np.uint8)
    else:
        c = by_word.astype(ml_dtypes.float4_e2m1fn).view(np.uint8) & 0xF
        words = (c[..., 0::2] | (c[..., 1::2] << 4)).reshape(k // 512, 128, 2 * n)
    return np.ascontiguousarray(words), np.ascontiguousarray(byte.astype(np.uint8).reshape(k // 512, 16, n))


def unpack_weight(words, scales, fmt):
    g, _, n = scales.shape
    words = np.ascontiguousarray(words).reshape(g, 128, n, -1)
    if fmt in ("e4m3", "e5m2"):
        vals = words.view(ml_dtypes.float8_e4m3fn if fmt == "e4m3" else ml_dtypes.float8_e5m2).astype(np.float64)
    else:
        nib = np.empty((g, 128, n, 4), np.uint8)
        nib[..., 0::2] = words & 0xF
        nib[..., 1::2] = words >> 4
        vals = E2M1[nib]
    vals = vals * np.repeat(np.exp2(scales.astype(np.float64) - 127.0), 8, axis=1)[..., None]
    return vals.transpose(0, 1, 3, 2).reshape(g * 512, n)


K, T, J, S, R, V, N = 1024, 1024, 256, 512, 512, 512, 256


def setup_inputs():
    n = np.random.standard_normal
    idx = np.random.permutation(T)[:J]
    idx2 = np.random.permutation(S)[:J]
    idx3 = np.random.permutation(V)[:J]
    fk = mx_kscale(K)
    fr = mx_kscale(R)
    wp = pack_weight(n((K, R)) * 1 / np.sqrt(K) * fk[:, None] * fr, "e5m2")
    wbp = pack_weight(n((R, N)) * 1 / np.sqrt(R) / fr[:, None], "e2m1")
    return {
        "xa": (n((K, T))).astype(np.float32),
        "xb": (n((K, S))).astype(np.float32),
        "hb": (np.random.uniform(0.2, 0.9, (K, 1))).astype(np.float32),
        "fk": (np.random.uniform(0.5, 2.0, (K, 1)) / fk[:, None]).astype(np.float32),
        "w_words": wp[0],
        "w_scales": wp[1],
        "tb": (n((R, V)) * 0.7 * fr[:, None]).astype(np.float32),
        "wb_words": wbp[0],
        "wb_scales": wbp[1],
        "rs": (1.0 * n((J, N))).astype(np.float32),
        "offs": striped(idx),
        "offs2": striped(idx2),
        "offs3": striped(idx3),
    }


def reference(xa, xb, hb, fk, w_words, w_scales, tb, wb_words, wb_scales, rs, offs, offs2, offs3):
    idx = unstriped(offs)
    idx2 = unstriped(offs2)
    idx3 = unstriped(offs3)
    wu = unpack_weight(w_words, w_scales, "e5m2")
    wbu = unpack_weight(wb_words, wb_scales, "e2m1")
    u = (f64(xa)[:, idx] - np.minimum(f64(xb)[:, idx2], f64(hb))) * f64(fk)
    uq = mxq(u, 0, "e5m2")
    a = wu.T @ uq
    hid = np.maximum(a - f64(tb)[:, idx3], 0.0)
    hidq = mxq(hid, 0, "e5m2")
    p = hidq.T @ wbu
    pk2 = np.max(np.abs(p), axis=1, keepdims=True)
    y = p / (pk2 + 0.2) + 0.3 * f64(rs)
    return y

@@ -1,0 +1,243 @@
+from contextlib import ExitStack
+
+import concourse.mybir as mybir
+
+K, T, J, S, R, V, N = 1024, 1024, 256, 512, 512, 512, 256
+FLOPS = 2 * K * R * J + 2 * J * R * N
+
+F32 = mybir.dt.float32
+BF16 = mybir.dt.bfloat16
+I32 = mybir.dt.int32
+U32 = mybir.dt.uint32
+U16 = mybir.dt.uint16
+U8 = mybir.dt.uint8
+E5M2X4 = mybir.dt.float8_e5m2_x4
+E2M1X4 = mybir.dt.float4_e2m1fn_x4
+ALU = mybir.AluOpType
+ACT = mybir.ActivationFunctionType
+
+P = 128
+PACK = 4
+PASSES = K // (P * PACK)
+HALF = 128
+HALVES = J // HALF
+PER_COL = 16
+QUADS = 4
+
+
+def tile_list_boundedgaps_overtable_rowpeaks_kernel(
+    tc, xa, xb, hb, fk, w_words, w_scales, tb, wb_words, wb_scales, rs, offs, offs2, offs3, out
+):
+    nc = tc.nc
+    xa_rows = xa.rearrange("(z p t) c -> z p t c", z=PASSES, t=PACK)
+    xb_rows = xb.rearrange("(z p t) c -> z p t c", z=PASSES, t=PACK)
+    tb_rows = tb.rearrange("(p t) c -> p t c", t=PACK)
+
+    with ExitStack() as ctx:
+        keep = ctx.enter_context(tc.tile_pool(name="keep", bufs=1))
+        psum = ctx.enter_context(tc.psum_pool(name="psum", bufs=1))
+
+        def sb(name, shape, dtype):
+            return keep.tile(shape, dtype, name=name, align_bytes=64)
+
+        list_a = sb("list_a", [P, J // PER_COL], U16)
+        list_b = sb("list_b", [P, J // PER_COL], U16)
+        list_t = sb("list_t", [P, J // PER_COL], U16)
+        xa_sb = {(z, t): sb("xa_%d_%d" % (z, t), [P, T], F32) for z in range(PASSES) for t in range(PACK)}
+        xb_sb = {(z, e): sb("xb_%d_%d" % (z, e), [P, 2, S], F32) for z in range(PASSES) for e in range(2)}
+        tb_sb = [sb("tb_%d" % t, [P, V], F32) for t in range(PACK)]
+        bound = sb("bound", [P, PASSES, 8], F32)
+        factor = sb("factor", [P, PASSES, 8], F32)
+        w_raw = sb("w_raw", [P, PASSES, R], I32)
+        w_codes = sb("w_codes", [P, PASSES, PACK, P], I32)
+        ws_raw = sb("ws_raw", [P, PASSES, R], U8)
+        w_plane = sb("w_plane", [P, PASSES, PACK, P], U8)
+        wb_codes = sb("wb_codes", [P, 2 * N], U8)
+        wb_plane = sb("wb_plane", [P, N], U8)
+        rs_sb = sb("rs_sb", [P, HALVES, N], F32)
+        rs_scaled = sb("rs_scaled", [P, HALVES, N], F32)
+        picked_t = sb("picked_t", [P, PACK, J], F32)
+        u_bf = [sb("u_bf_%d" % z, [P, J, PACK], BF16) for z in range(PASSES)]
+        u_codes = [sb("u_codes_%d" % z, [P, J], U32) for z in range(PASSES)]
+        u_plane = [sb("u_plane_%d" % z, [P, J], U8) for z in range(PASSES)]
+        a_bank = [psum.tile([P, PACK, HALF], F32, name="a_bank_%d" % h) for h in range(HALVES)]
+        p_bank = [psum.tile([P, N], F32, name="p_bank_%d" % h) for h in range(HALVES)]
+
+        def gather(engine, dst, window, offsets):
+            if engine == "scalar":
+                nc.scalar.activation(dst, window.indirect(offsets), ACT.Copy)
+            else:
+                nc.vector.tensor_copy(dst, window.indirect(offsets))
+
+        def load_xa(z, t):
+            nc.sync.dma_start(xa_sb[z, t][:], xa_rows[z, :, t, :])
+
+        def load_xb(z, e):
+            nc.sync.dma_start(xb_sb[z, e][:], xb_rows[z, :, 2 * e : 2 * e + 2, :])
+
+        def load_tb(t):
+            nc.sync.dma_start(tb_sb[t][:], tb_rows[:, t, :])
+
+        def load_w_scale(q):
+            nc.sync.dma_start(
+                ws_raw[32 * q : 32 * q + 4, :, :].bitcast(I32),
+                w_scales[:, 4 * q : 4 * q + 4, :].rearrange("z r c -> r z c").bitcast(I32),
+            )
+
+        def load_wb_scale(q):
+            nc.sync.dma_start(
+                wb_plane[32 * q : 32 * q + 4, :].bitcast(I32), wb_scales[0, 4 * q : 4 * q + 4, :].bitcast(I32)
+            )
+
+        picked_b = {}
+
+        def pick_b(z, t):
+            picked_b[z, t] = sb("picked_b_%d_%d" % (z, t), [P, J], F32)
+            gather("scalar" if t % 2 == 0 else "vector", picked_b[z, t][:], xb_sb[z, t // 2][:, t % 2, :], list_b[:])
+
+        def make_u(z, t, parts):
+            picked_a = sb("picked_a_%d_%d" % (z, t), [P, J], F32)
+            gap = sb("gap_%d_%d" % (z, t), [P, J], F32)
+            for lo, hi in parts:
+                gather("scalar", picked_a[:, lo:hi], xa_sb[z, t][:], list_a[:, lo // PER_COL : hi // PER_COL])
+            for lo, hi in parts:
+                nc.vector.scalar_tensor_tensor(
+                    gap[:, lo:hi], picked_b[z, t][:, lo:hi], bound[:, z, t : t + 1], picked_a[:, lo:hi],
+                    ALU.min, ALU.subtract,
+                )
+            for lo, hi in parts:
+                nc.vector.tensor_scalar(
+                    u_bf[z][:, lo:hi, t], gap[:, lo:hi], factor[:, z, t : t + 1], -1.0, ALU.mult, ALU.mult
+                )
+
+        def quantize_u(z, lo, hi):
+            nc.vector.quantize_mx(
+                out=u_codes[z][:, lo:hi].bitcast(E5M2X4),
+                scales=u_plane[z][:, lo:hi],
+                in_=u_bf[z][:, lo:hi, :].rearrange("p j t -> p (j t)"),
+            )
+
+        def first_product(z, h):
+            cols = slice(h * HALF, (h + 1) * HALF)
+            for t in range(PACK):
+                nc.tensor.matmul_mx(
+                    out=a_bank[h][:, t, :],
+                    lhsT=w_codes[:, z, t, :].bitcast(E5M2X4),
+                    lhsT_scale=w_plane[:, z, t, :],
+                    rhs=u_codes[z][:, cols].bitcast(E5M2X4),
+                    rhs_scale=u_plane[z][:, cols],
+                    start=(z == 0 and t == 0),
+                    stop=(z == PASSES - 1 and t == PACK - 1),
+                )
+
+        def pick_t(t, h):
+            gather(
+                "scalar", picked_t[:, t, h * HALF : (h + 1) * HALF], tb_sb[t][:],
+                list_t[:, h * HALF // PER_COL : (h + 1) * HALF // PER_COL],
+            )
+
+        whole = [(0, J)]
+        halves = [(h * HALF, (h + 1) * HALF) for h in range(HALVES)]
+
+        nc.gpsimd.memset(ws_raw[:].rearrange("p z c -> p (z c)").bitcast(U32), 0)
+        nc.gpsimd.memset(wb_plane[:].bitcast(U32), 0)
+
+        load_xb(0, 0)
+        nc.sync.dma_start(list_b[:], offs2)
+        load_xa(0, 0)
+        nc.sync.dma_start(list_a[:], offs)
+        nc.sync.dma_start(bound[:, :, 0:PACK], hb.rearrange("(z p t) o -> p z (t o)", z=PASSES, t=PACK))
+        nc.sync.dma_start(factor[:, :, 0:PACK], fk.rearrange("(z p t) o -> p z (t o)", z=PASSES, t=PACK))
+        load_xa(0, 1)
+        load_w_scale(0)
+        load_xb(0, 1)
+        load_w_scale(1)
+        load_xa(0, 2)
+        load_w_scale(2)
+        load_xa(0, 3)
+        load_w_scale(3)
+        nc.sync.dma_start(w_raw[:], w_words.rearrange("z p c r -> p z (c r)").bitcast(I32))
+        nc.sync.dma_start(list_t[:], offs3)
+        load_xb(1, 0)
+        load_wb_scale(0)
+        load_xa(1, 0)
+        load_wb_scale(1)
+        load_xa(1, 1)
+        load_wb_scale(2)
+        load_xb(1, 1)
+        load_wb_scale(3)
+        load_xa(1, 2)
+        load_xa(1, 3)
+        for t in range(PACK):
+            load_tb(t)
+        nc.sync.dma_start(wb_codes[:], wb_words[0])
+        nc.sync.dma_start(rs_sb[:], rs.rearrange("(h p) n -> p h n", p=P))
+
+        for e in range(2):
+            pick_b(0, 2 * e)
+            pick_b(0, 2 * e + 1)
+            make_u(0, 2 * e, whole)
+            make_u(0, 2 * e + 1, whole)
+        nc.vector.tensor_copy(
+            w_plane[:].rearrange("p z t m -> p z m t"), ws_raw[:].rearrange("p z (m t) -> p z m t", t=PACK)
+        )
+        quantize_u(0, 0, J)
+        nc.vector.tensor_copy(
+            w_codes[:].rearrange("p z t m -> p z m t"), w_raw[:].rearrange("p z (m t) -> p z m t", t=PACK)
+        )
+        for h in range(HALVES):
+            first_product(0, h)
+        pick_b(1, 0)
+        pick_b(1, 1)
+        make_u(1, 0, whole)
+        make_u(1, 1, whole)
+        pick_b(1, 2)
+        pick_b(1, 3)
+        make_u(1, 2, whole)
+        make_u(1, 3, halves)
+        for h in range(HALVES):
+            quantize_u(1, h * HALF, (h + 1) * HALF)
+            first_product(1, h)
+        for h in range(HALVES):
+            for t in range(PACK):
+                pick_t(t, h)
+        nc.scalar.activation(rs_scaled[:], rs_sb[:], ACT.Copy, scale=0.3)
+
+        over = [sb("over_%d" % h, [P, HALF, PACK], BF16) for h in range(HALVES)]
+        hid = [sb("hid_%d" % h, [P, HALF * PACK], BF16) for h in range(HALVES)]
+        hid_codes = [sb("hid_codes_%d" % h, [P, HALF], U32) for h in range(HALVES)]
+        hid_plane = [sb("hid_plane_%d" % h, [P, HALF], U8) for h in range(HALVES)]
+        size = [sb("size_%d" % h, [P, N], F32) for h in range(HALVES)]
+        shifted = [sb("shifted_%d" % h, [P, N], F32) for h in range(HALVES)]
+        divisor = [sb("divisor_%d" % h, [P, 1], F32) for h in range(HALVES)]
+        inverse = [sb("inverse_%d" % h, [P, 1], F32) for h in range(HALVES)]
+        result = [sb("result_%d" % h, [P, N], F32) for h in range(HALVES)]
+
+        for h in range(HALVES):
+            nc.vector.tensor_tensor(
+                over[h][:].rearrange("p (c i) t -> p c t i", i=4),
+                a_bank[h][:].rearrange("p t (c i) -> p c t i", i=4),
+                picked_t[:, :, h * HALF : (h + 1) * HALF].rearrange("p t (c i) -> p c t i", i=4),
+                ALU.subtract,
+            )
+            nc.vector.tensor_scalar(hid[h][:], over[h][:].rearrange("p j t -> p (j t)"), 0.0, None, ALU.max)
+            nc.vector.quantize_mx(out=hid_codes[h][:].bitcast(E5M2X4), scales=hid_plane[h][:], in_=hid[h][:])
+            nc.tensor.matmul_mx(
+                out=p_bank[h][:],
+                lhsT=hid_codes[h][:].bitcast(E5M2X4),
+                lhsT_scale=hid_plane[h][:],
+                rhs=wb_codes[:].bitcast(E2M1X4),
+                rhs_scale=wb_plane[:],
+                start=True,
+                stop=True,
+            )
+            nc.scalar.activation(size[h][:], p_bank[h][:], ACT.Abs)
+        for h in range(HALVES):
+            nc.vector.tensor_scalar(
+                shifted[h][:], size[h][:], 0.2, None, ALU.add, ALU.max, accum_out=divisor[h][:]
+            )
+            nc.vector.reciprocal(inverse[h][:], divisor[h][:])
+            nc.vector.scalar_tensor_tensor(
+                result[h][:], p_bank[h][:], inverse[h][:], rs_scaled[:, h, :], ALU.mult, ALU.add
+            )
+            nc.sync.dma_start(out[h * HALF : (h + 1) * HALF, :], result[h][:])

@@ -1,6 +1,7 @@
 from contextlib import ExitStack
 
 import concourse.mybir as mybir
+from concourse.masks import make_identity
 
 K, T, J, S, R, V, N = 1024, 1024, 256, 512, 512, 512, 256
 FLOPS = 2 * K * R * J + 2 * J * R * N
@@ -37,17 +38,20 @@ def tile_list_boundedgaps_overtable_rowpeaks_kernel(
         keep = ctx.enter_context(tc.tile_pool(name="keep", bufs=1))
         psum = ctx.enter_context(tc.psum_pool(name="psum", bufs=1))
 
-        def sb(name, shape, dtype):
-            return keep.tile(shape, dtype, name=name, align_bytes=64)
+        def sb(name, shape, dtype, tag=None):
+            return keep.tile(shape, dtype, name=name, tag=tag or name, align_bytes=64)
 
         list_a = sb("list_a", [P, J // PER_COL], U16)
         list_b = sb("list_b", [P, J // PER_COL], U16)
         list_t = sb("list_t", [P, J // PER_COL], U16)
-        xa_sb = {(z, t): sb("xa_%d_%d" % (z, t), [P, T], F32) for z in range(PASSES) for t in range(PACK)}
-        xb_sb = {(z, e): sb("xb_%d_%d" % (z, e), [P, 2, S], F32) for z in range(PASSES) for e in range(2)}
-        tb_sb = [sb("tb_%d" % t, [P, V], F32) for t in range(PACK)]
-        bound = sb("bound", [P, PASSES, 8], F32)
-        factor = sb("factor", [P, PASSES, 8], F32)
+        xa_pair = [sb("xa_pair_%d" % e, [P, 2, T], F32) for e in range(2)]
+        xa_single = [sb("xa_single_%d" % t, [P, T], F32) for t in range(PACK)]
+        xb_sb = [sb("xb_%d" % z, [P, PACK, S], F32) for z in range(PASSES)]
+        tb_sb = [sb("tb_%d" % e, [P, 2, V], F32) for e in range(2)]
+        vec_rows = sb("vec_rows", [P, P * PACK], F32)
+        ident = sb("ident", [P, P], F32)
+        vec_cols = sb("vec_cols", [P, PACK, 2 * PASSES], F32)
+        vec_bank = psum.tile([P, PACK, P], F32, name="vec_bank")
         w_raw = sb("w_raw", [P, PASSES, R], I32)
         w_codes = sb("w_codes", [P, PASSES, PACK, P], I32)
         ws_raw = sb("ws_raw", [P, PASSES, R], U8)
@@ -69,14 +73,14 @@ def tile_list_boundedgaps_overtable_rowpeaks_kernel(
             else:
                 nc.vector.tensor_copy(dst, window.indirect(offsets))
 
-        def load_xa(z, t):
-            nc.sync.dma_start(xa_sb[z, t][:], xa_rows[z, :, t, :])
+        def xa_window(z, t):
+            return xa_pair[t // 2][:, t % 2, :] if z == 0 else xa_single[t][:]
 
-        def load_xb(z, e):
-            nc.sync.dma_start(xb_sb[z, e][:], xb_rows[z, :, 2 * e : 2 * e + 2, :])
+        def bound(z, t):
+            return vec_cols[:, t, z : z + 1]
 
-        def load_tb(t):
-            nc.sync.dma_start(tb_sb[t][:], tb_rows[:, t, :])
+        def factor(z, t):
+            return vec_cols[:, t, PASSES + z : PASSES + z + 1]
 
         def load_w_scale(q):
             nc.sync.dma_start(
@@ -93,22 +97,28 @@ def tile_list_boundedgaps_overtable_rowpeaks_kernel(
 
         def pick_b(z, t):
             picked_b[z, t] = sb("picked_b_%d_%d" % (z, t), [P, J], F32)
-            gather("scalar" if t % 2 == 0 else "vector", picked_b[z, t][:], xb_sb[z, t // 2][:, t % 2, :], list_b[:])
+            gather("scalar" if t % 2 == 0 else "vector", picked_b[z, t][:], xb_sb[z][:, t, :], list_b[:])
 
-        def make_u(z, t, parts):
+        def make_u(z, t):
             picked_a = sb("picked_a_%d_%d" % (z, t), [P, J], F32)
             gap = sb("gap_%d_%d" % (z, t), [P, J], F32)
-            for lo, hi in parts:
-                gather("scalar", picked_a[:, lo:hi], xa_sb[z, t][:], list_a[:, lo // PER_COL : hi // PER_COL])
-            for lo, hi in parts:
+            gather("scalar", picked_a[:], xa_window(z, t), list_a[:])
+            nc.vector.scalar_tensor_tensor(
+                gap[:], picked_b[z, t][:], bound(z, t), picked_a[:], ALU.min, ALU.subtract
+            )
+            nc.vector.tensor_scalar(u_bf[z][:, :, t], gap[:], factor(z, t), -1.0, ALU.mult, ALU.mult)
+
+        def make_last_u(z, t):
+            picked_a = sb("picked_a_last", [P, J], F32)
+            gap = sb("gap_last", [P, J], F32, tag="w_raw")
+            for lo, hi in halves:
+                gather("scalar", picked_a[:, lo:hi], xa_window(z, t), list_a[:, lo // PER_COL : hi // PER_COL])
+            for lo, hi in halves:
                 nc.vector.scalar_tensor_tensor(
-                    gap[:, lo:hi], picked_b[z, t][:, lo:hi], bound[:, z, t : t + 1], picked_a[:, lo:hi],
-                    ALU.min, ALU.subtract,
+                    gap[:, lo:hi], picked_b[z, t][:, lo:hi], bound(z, t), picked_a[:, lo:hi], ALU.min, ALU.subtract
                 )
-            for lo, hi in parts:
-                nc.vector.tensor_scalar(
-                    u_bf[z][:, lo:hi, t], gap[:, lo:hi], factor[:, z, t : t + 1], -1.0, ALU.mult, ALU.mult
-                )
+            for lo, hi in halves:
+                nc.vector.tensor_scalar(u_bf[z][:, lo:hi, t], gap[:, lo:hi], factor(z, t), -1.0, ALU.mult, ALU.mult)
 
         def quantize_u(z, lo, hi):
             nc.vector.quantize_mx(
@@ -132,75 +142,73 @@ def tile_list_boundedgaps_overtable_rowpeaks_kernel(
 
         def pick_t(t, h):
             gather(
-                "scalar", picked_t[:, t, h * HALF : (h + 1) * HALF], tb_sb[t][:],
+                "vector" if t == PACK - 1 else "scalar",
+                picked_t[:, t, h * HALF : (h + 1) * HALF], tb_sb[t // 2][:, t % 2, :],
                 list_t[:, h * HALF // PER_COL : (h + 1) * HALF // PER_COL],
             )
 
-        whole = [(0, J)]
         halves = [(h * HALF, (h + 1) * HALF) for h in range(HALVES)]
 
-        nc.gpsimd.memset(ws_raw[:].rearrange("p z c -> p (z c)").bitcast(U32), 0)
+        nc.vector.memset(vec_rows[:], 0.0)
+        nc.vector.memset(ws_raw[:].rearrange("p z c -> p (z c)").bitcast(U32), 0)
+        make_identity(nc, ident[:])
         nc.gpsimd.memset(wb_plane[:].bitcast(U32), 0)
 
-        load_xb(0, 0)
+        nc.sync.dma_start(xb_sb[0][:], xb_rows[0])
         nc.sync.dma_start(list_b[:], offs2)
-        load_xa(0, 0)
+        nc.sync.dma_start(vec_rows[0:PASSES, :], hb.rearrange("(z c) o -> z (c o)", z=PASSES))
+        nc.sync.dma_start(vec_rows[PASSES : 2 * PASSES, :], fk.rearrange("(z c) o -> z (c o)", z=PASSES))
+        nc.sync.dma_start(xa_pair[0][:], xa_rows[0, :, 0:2, :])
         nc.sync.dma_start(list_a[:], offs)
-        nc.sync.dma_start(bound[:, :, 0:PACK], hb.rearrange("(z p t) o -> p z (t o)", z=PASSES, t=PACK))
-        nc.sync.dma_start(factor[:, :, 0:PACK], fk.rearrange("(z p t) o -> p z (t o)", z=PASSES, t=PACK))
-        load_xa(0, 1)
         load_w_scale(0)
-        load_xb(0, 1)
         load_w_scale(1)
-        load_xa(0, 2)
+        nc.sync.dma_start(xa_pair[1][:], xa_rows[0, :, 2:4, :])
         load_w_scale(2)
-        load_xa(0, 3)
         load_w_scale(3)
-        nc.sync.dma_start(w_raw[:], w_words.rearrange("z p c r -> p z (c r)").bitcast(I32))
+        nc.sync.dma_start(xb_sb[1][:], xb_rows[1])
         nc.sync.dma_start(list_t[:], offs3)
-        load_xb(1, 0)
-        load_wb_scale(0)
-        load_xa(1, 0)
-        load_wb_scale(1)
-        load_xa(1, 1)
-        load_wb_scale(2)
-        load_xb(1, 1)
-        load_wb_scale(3)
-        load_xa(1, 2)
-        load_xa(1, 3)
-        for t in range(PACK):
-            load_tb(t)
+        nc.sync.dma_start(xa_single[0][:], xa_rows[1, :, 0, :])
+        nc.sync.dma_start(xa_single[1][:], xa_rows[1, :, 1, :])
+        nc.sync.dma_start(xa_single[2][:], xa_rows[1, :, 2, :])
+        nc.sync.dma_start(w_raw[:], w_words.rearrange("z p c r -> p z (c r)").bitcast(I32))
+        nc.sync.dma_start(xa_single[3][:], xa_rows[1, :, 3, :])
+        for e in range(2):
+            nc.sync.dma_start(tb_sb[e][:], tb_rows[:, 2 * e : 2 * e + 2, :])
         nc.sync.dma_start(wb_codes[:], wb_words[0])
+        for q in range(QUADS):
+            load_wb_scale(q)
         nc.sync.dma_start(rs_sb[:], rs.rearrange("(h p) n -> p h n", p=P))
 
-        for e in range(2):
-            pick_b(0, 2 * e)
-            pick_b(0, 2 * e + 1)
-            make_u(0, 2 * e, whole)
-            make_u(0, 2 * e + 1, whole)
+        for t in range(PACK):
+            nc.tensor.transpose(vec_bank[:, t, :], vec_rows[:, t :: PACK], ident[:])
+        nc.vector.tensor_copy(vec_cols[:], vec_bank[:, :, 0 : 2 * PASSES])
+
+        for t in range(PACK):
+            pick_b(0, t)
+        for t in range(PACK):
+            make_u(0, t)
         nc.vector.tensor_copy(
             w_plane[:].rearrange("p z t m -> p z m t"), ws_raw[:].rearrange("p z (m t) -> p z m t", t=PACK)
         )
         quantize_u(0, 0, J)
+        for t in range(PACK):
+            pick_b(1, t)
+        make_u(1, 0)
+        make_u(1, 1)
+        make_u(1, 2)
         nc.vector.tensor_copy(
             w_codes[:].rearrange("p z t m -> p z m t"), w_raw[:].rearrange("p z (m t) -> p z m t", t=PACK)
         )
         for h in range(HALVES):
             first_product(0, h)
-        pick_b(1, 0)
-        pick_b(1, 1)
-        make_u(1, 0, whole)
-        make_u(1, 1, whole)
-        pick_b(1, 2)
-        pick_b(1, 3)
-        make_u(1, 2, whole)
-        make_u(1, 3, halves)
+        make_last_u(1, 3)
         for h in range(HALVES):
             quantize_u(1, h * HALF, (h + 1) * HALF)
             first_product(1, h)
-        for h in range(HALVES):
-            for t in range(PACK):
-                pick_t(t, h)
+        for e in range(2):
+            for h in range(HALVES):
+                for t in (2 * e, 2 * e + 1):
+                    pick_t(t, h)
         nc.scalar.activation(rs_scaled[:], rs_sb[:], ACT.Copy, scale=0.3)
 
         over = [sb("over_%d" % h, [P, HALF, PACK], BF16) for h in range(HALVES)]

@@ -44,13 +44,17 @@ def tile_list_boundedgaps_overtable_rowpeaks_kernel(
         list_a = sb("list_a", [P, J // PER_COL], U16)
         list_b = sb("list_b", [P, J // PER_COL], U16)
         list_t = sb("list_t", [P, J // PER_COL], U16)
-        xa_pair = [sb("xa_pair_%d" % e, [P, 2, T], F32) for e in range(2)]
-        xa_single = [sb("xa_single_%d" % t, [P, T], F32) for t in range(PACK)]
-        xb_sb = [sb("xb_%d" % z, [P, PACK, S], F32) for z in range(PASSES)]
+        xa_loads = [(0, 0, 1), (0, 1, 2), (0, 2, 4), (1, 0, 1), (1, 1, 2), (1, 2, 3), (1, 3, 4)]
+        xb_loads = [(0, 0, 2), (0, 2, 4), (1, 0, 3), (1, 3, 4)]
+        xa_sb = {k: sb("xa_%d_%d" % k[:2], [P, k[2] - k[1], T], F32) for k in xa_loads}
+        xb_sb = {k: sb("xb_%d_%d" % k[:2], [P, k[2] - k[1], S], F32) for k in xb_loads}
         tb_sb = [sb("tb_%d" % e, [P, 2, V], F32) for e in range(2)]
         vec_rows = sb("vec_rows", [P, P * PACK], F32)
         ident = sb("ident", [P, P], F32)
-        vec_cols = sb("vec_cols", [P, PACK, 2 * PASSES], F32)
+        bounds = sb("bounds", [P, PACK, PASSES], F32)
+        neg_factors = sb("neg_factors", [P, PACK, PASSES], F32)
+        table_warm = sb("table_warm", [P, 2], F32)
+        gap_first = sb("gap_first", [P, PACK, J], F32)
         vec_bank = psum.tile([P, PACK, P], F32, name="vec_bank")
         w_raw = sb("w_raw", [P, PASSES, R], I32)
         w_codes = sb("w_codes", [P, PASSES, PACK, P], I32)
@@ -62,7 +66,7 @@ def tile_list_boundedgaps_overtable_rowpeaks_kernel(
         rs_scaled = sb("rs_scaled", [P, HALVES, N], F32)
         picked_t = sb("picked_t", [P, PACK, J], F32)
         u_bf = [sb("u_bf_%d" % z, [P, J, PACK], BF16) for z in range(PASSES)]
-        u_codes = [sb("u_codes_%d" % z, [P, J], U32) for z in range(PASSES)]
+        u_codes = {1: sb("u_codes_1", [P, J], U32)}
         u_plane = [sb("u_plane_%d" % z, [P, J], U8) for z in range(PASSES)]
         a_bank = [psum.tile([P, PACK, HALF], F32, name="a_bank_%d" % h) for h in range(HALVES)]
         p_bank = [psum.tile([P, N], F32, name="p_bank_%d" % h) for h in range(HALVES)]
@@ -73,14 +77,19 @@ def tile_list_boundedgaps_overtable_rowpeaks_kernel(
             else:
                 nc.vector.tensor_copy(dst, window.indirect(offsets))
 
-        def xa_window(z, t):
-            return xa_pair[t // 2][:, t % 2, :] if z == 0 else xa_single[t][:]
+        def window(tiles, z, t):
+            key = [k for k in tiles if k[0] == z and k[1] <= t < k[2]][0]
+            return tiles[key][:, t - key[1], :]
+
+        def load(tiles, rows, z, t):
+            key = [k for k in tiles if k[:2] == (z, t)][0]
+            nc.sync.dma_start(tiles[key][:], rows[z, :, key[1] : key[2], :])
 
         def bound(z, t):
-            return vec_cols[:, t, z : z + 1]
+            return bounds[:, t, z : z + 1]
 
-        def factor(z, t):
-            return vec_cols[:, t, PASSES + z : PASSES + z + 1]
+        def neg_factor(z, t):
+            return neg_factors[:, t, z : z + 1]
 
         def load_w_scale(q):
             nc.sync.dma_start(
@@ -97,28 +106,22 @@ def tile_list_boundedgaps_overtable_rowpeaks_kernel(
 
         def pick_b(z, t):
             picked_b[z, t] = sb("picked_b_%d_%d" % (z, t), [P, J], F32)
-            gather("scalar" if t % 2 == 0 else "vector", picked_b[z, t][:], xb_sb[z][:, t, :], list_b[:])
+            gather("vector" if t == 1 else "scalar", picked_b[z, t][:], window(xb_sb, z, t), list_b[:])
 
-        def make_u(z, t):
+        def make_gap(z, t, gap, parts):
             picked_a = sb("picked_a_%d_%d" % (z, t), [P, J], F32)
-            gap = sb("gap_%d_%d" % (z, t), [P, J], F32)
-            gather("scalar", picked_a[:], xa_window(z, t), list_a[:])
-            nc.vector.scalar_tensor_tensor(
-                gap[:], picked_b[z, t][:], bound(z, t), picked_a[:], ALU.min, ALU.subtract
-            )
-            nc.vector.tensor_scalar(u_bf[z][:, :, t], gap[:], factor(z, t), -1.0, ALU.mult, ALU.mult)
-
-        def make_last_u(z, t):
-            picked_a = sb("picked_a_last", [P, J], F32)
-            gap = sb("gap_last", [P, J], F32, tag="w_raw")
-            for lo, hi in halves:
-                gather("scalar", picked_a[:, lo:hi], xa_window(z, t), list_a[:, lo // PER_COL : hi // PER_COL])
-            for lo, hi in halves:
+            for lo, hi in parts:
+                gather("scalar", picked_a[:, lo:hi], window(xa_sb, z, t), list_a[:, lo // PER_COL : hi // PER_COL])
+            for lo, hi in parts:
                 nc.vector.scalar_tensor_tensor(
                     gap[:, lo:hi], picked_b[z, t][:, lo:hi], bound(z, t), picked_a[:, lo:hi], ALU.min, ALU.subtract
                 )
-            for lo, hi in halves:
-                nc.vector.tensor_scalar(u_bf[z][:, lo:hi, t], gap[:, lo:hi], factor(z, t), -1.0, ALU.mult, ALU.mult)
+
+        def make_u(z, t, parts):
+            gap = sb("gap_%d_%d" % (z, t), [P, J], F32)
+            make_gap(z, t, gap, parts)
+            for lo, hi in parts:
+                nc.vector.tensor_scalar(u_bf[z][:, lo:hi, t], gap[:, lo:hi], neg_factor(z, t), None, ALU.mult)
 
         def quantize_u(z, lo, hi):
             nc.vector.quantize_mx(
@@ -140,38 +143,40 @@ def tile_list_boundedgaps_overtable_rowpeaks_kernel(
                     stop=(z == PASSES - 1 and t == PACK - 1),
                 )
 
-        def pick_t(t, h):
+        def pick_t(t, lo, hi):
             gather(
                 "vector" if t == PACK - 1 else "scalar",
-                picked_t[:, t, h * HALF : (h + 1) * HALF], tb_sb[t // 2][:, t % 2, :],
-                list_t[:, h * HALF // PER_COL : (h + 1) * HALF // PER_COL],
+                picked_t[:, t, lo:hi], tb_sb[t // 2][:, t % 2, :], list_t[:, lo // PER_COL : hi // PER_COL],
             )
 
         halves = [(h * HALF, (h + 1) * HALF) for h in range(HALVES)]
 
+        whole = [(0, J)]
+        nc.vector.memset(table_warm[:, 0:1], 0.0)
+        nc.scalar.activation(table_warm[:, 1:2], table_warm[:, 0:1], ACT.Copy)
         nc.vector.memset(vec_rows[:], 0.0)
         nc.vector.memset(ws_raw[:].rearrange("p z c -> p (z c)").bitcast(U32), 0)
         make_identity(nc, ident[:])
         nc.gpsimd.memset(wb_plane[:].bitcast(U32), 0)
 
-        nc.sync.dma_start(xb_sb[0][:], xb_rows[0])
+        load(xb_sb, xb_rows, 0, 0)
         nc.sync.dma_start(list_b[:], offs2)
-        nc.sync.dma_start(vec_rows[0:PASSES, :], hb.rearrange("(z c) o -> z (c o)", z=PASSES))
-        nc.sync.dma_start(vec_rows[PASSES : 2 * PASSES, :], fk.rearrange("(z c) o -> z (c o)", z=PASSES))
-        nc.sync.dma_start(xa_pair[0][:], xa_rows[0, :, 0:2, :])
+        nc.sync.dma_start(vec_rows[4:12:4, :], hb.rearrange("(z c) o -> z (c o)", z=PASSES))
+        nc.sync.dma_start(vec_rows[12:20:4, :], fk.rearrange("(z c) o -> z (c o)", z=PASSES))
+        load(xa_sb, xa_rows, 0, 0)
         nc.sync.dma_start(list_a[:], offs)
-        load_w_scale(0)
-        load_w_scale(1)
-        nc.sync.dma_start(xa_pair[1][:], xa_rows[0, :, 2:4, :])
-        load_w_scale(2)
-        load_w_scale(3)
-        nc.sync.dma_start(xb_sb[1][:], xb_rows[1])
-        nc.sync.dma_start(list_t[:], offs3)
-        nc.sync.dma_start(xa_single[0][:], xa_rows[1, :, 0, :])
-        nc.sync.dma_start(xa_single[1][:], xa_rows[1, :, 1, :])
-        nc.sync.dma_start(xa_single[2][:], xa_rows[1, :, 2, :])
+        load(xa_sb, xa_rows, 0, 1)
+        load(xb_sb, xb_rows, 0, 2)
+        for q in range(QUADS):
+            load_w_scale(q)
+        load(xa_sb, xa_rows, 0, 2)
         nc.sync.dma_start(w_raw[:], w_words.rearrange("z p c r -> p z (c r)").bitcast(I32))
-        nc.sync.dma_start(xa_single[3][:], xa_rows[1, :, 3, :])
+        load(xb_sb, xb_rows, 1, 0)
+        nc.sync.dma_start(list_t[:], offs3)
+        for t in range(PACK - 1):
+            load(xa_sb, xa_rows, 1, t)
+        load(xb_sb, xb_rows, 1, PACK - 1)
+        load(xa_sb, xa_rows, 1, PACK - 1)
         for e in range(2):
             nc.sync.dma_start(tb_sb[e][:], tb_rows[:, 2 * e : 2 * e + 2, :])
         nc.sync.dma_start(wb_codes[:], wb_words[0])
@@ -181,34 +186,45 @@ def tile_list_boundedgaps_overtable_rowpeaks_kernel(
 
         for t in range(PACK):
             nc.tensor.transpose(vec_bank[:, t, :], vec_rows[:, t :: PACK], ident[:])
-        nc.vector.tensor_copy(vec_cols[:], vec_bank[:, :, 0 : 2 * PASSES])
+        nc.vector.tensor_copy(bounds[:], vec_bank[:, :, 4:12:4])
+        nc.vector.tensor_scalar(neg_factors[:], vec_bank[:, :, 12:20:4], -1.0, None, ALU.mult)
 
-        for t in range(PACK):
-            pick_b(0, t)
-        for t in range(PACK):
-            make_u(0, t)
+        for e in range(2):
+            for t in (2 * e, 2 * e + 1):
+                pick_b(0, t)
+            for t in (2 * e, 2 * e + 1):
+                make_gap(0, t, gap_first[:, t, :], whole)
         nc.vector.tensor_copy(
             w_plane[:].rearrange("p z t m -> p z m t"), ws_raw[:].rearrange("p z (m t) -> p z m t", t=PACK)
         )
-        quantize_u(0, 0, J)
-        for t in range(PACK):
-            pick_b(1, t)
-        make_u(1, 0)
-        make_u(1, 1)
-        make_u(1, 2)
+        nc.vector.tensor_tensor(
+            u_bf[0][:].rearrange("p (c i) t -> p c t i", i=4),
+            gap_first[:].rearrange("p t (c i) -> p c t i", i=4),
+            neg_factors[:, :, 0:1].unsqueeze(1).to_broadcast([P, J // 4, PACK, 4]),
+            ALU.mult,
+        )
         nc.vector.tensor_copy(
             w_codes[:].rearrange("p z t m -> p z m t"), w_raw[:].rearrange("p z (m t) -> p z m t", t=PACK)
         )
+        for t in range(PACK - 1):
+            pick_b(1, t)
+        make_u(1, 0, whole)
+        make_u(1, 1, whole)
+        u_codes[0] = sb("u_codes_0", [P, J], U32, tag="gap_1_1")
+        quantize_u(0, 0, J)
         for h in range(HALVES):
             first_product(0, h)
-        make_last_u(1, 3)
+        make_u(1, 2, whole)
+        pick_b(1, 3)
+        make_u(1, 3, halves)
         for h in range(HALVES):
             quantize_u(1, h * HALF, (h + 1) * HALF)
             first_product(1, h)
-        for e in range(2):
-            for h in range(HALVES):
-                for t in (2 * e, 2 * e + 1):
-                    pick_t(t, h)
+        for t in (0, 1):
+            pick_t(t, 0, J)
+        for lo, hi in halves:
+            for t in (2, 3):
+                pick_t(t, lo, hi)
         nc.scalar.activation(rs_scaled[:], rs_sb[:], ACT.Copy, scale=0.3)
 
         over = [sb("over_%d" % h, [P, HALF, PACK], BF16) for h in range(HALVES)]

@@ -24,6 +24,17 @@ HALF = 128
 HALVES = J // HALF
 PER_COL = 16
 QUADS = 4
+RUN = 4
+WHOLE = [(0, J)]
+IN_HALVES = [(h * HALF, (h + 1) * HALF) for h in range(HALVES)]
+
+XA_LOADS = [(0, 0, 1), (0, 1, 2), (0, 2, 4), (1, 0, 1), (1, 1, 2), (1, 2, 3), (1, 3, 4)]
+XB_LOADS = [(0, 0, 2), (0, 2, 4), (1, 0, 3), (1, 3, 4)]
+TB_LOADS = [(0, 0, 2), (0, 2, 4)]
+XB_PLANE_ON_VECTOR = 1
+TB_PLANE_ON_VECTOR = PACK - 1
+HB_ROWS = slice(4, 12, 4)
+FK_ROWS = slice(12, 20, 4)
 
 
 def tile_list_boundedgaps_overtable_rowpeaks_kernel(
@@ -32,7 +43,7 @@ def tile_list_boundedgaps_overtable_rowpeaks_kernel(
     nc = tc.nc
     xa_rows = xa.rearrange("(z p t) c -> z p t c", z=PASSES, t=PACK)
     xb_rows = xb.rearrange("(z p t) c -> z p t c", z=PASSES, t=PACK)
-    tb_rows = tb.rearrange("(p t) c -> p t c", t=PACK)
+    tb_rows = tb.rearrange("(z p t) c -> z p t c", z=1, t=PACK)
 
     with ExitStack() as ctx:
         keep = ctx.enter_context(tc.tile_pool(name="keep", bufs=1))
@@ -44,89 +55,79 @@ def tile_list_boundedgaps_overtable_rowpeaks_kernel(
         list_a = sb("list_a", [P, J // PER_COL], U16)
         list_b = sb("list_b", [P, J // PER_COL], U16)
         list_t = sb("list_t", [P, J // PER_COL], U16)
-        xa_loads = [(0, 0, 1), (0, 1, 2), (0, 2, 4), (1, 0, 1), (1, 1, 2), (1, 2, 3), (1, 3, 4)]
-        xb_loads = [(0, 0, 2), (0, 2, 4), (1, 0, 3), (1, 3, 4)]
-        xa_sb = {k: sb("xa_%d_%d" % k[:2], [P, k[2] - k[1], T], F32) for k in xa_loads}
-        xb_sb = {k: sb("xb_%d_%d" % k[:2], [P, k[2] - k[1], S], F32) for k in xb_loads}
-        tb_sb = [sb("tb_%d" % e, [P, 2, V], F32) for e in range(2)]
+        xa_sb = {k: sb("xa_%d_%d" % k[:2], [P, k[2] - k[1], T], F32) for k in XA_LOADS}
+        xb_sb = {k: sb("xb_%d_%d" % k[:2], [P, k[2] - k[1], S], F32) for k in XB_LOADS}
+        tb_sb = {k: sb("tb_%d_%d" % k[:2], [P, k[2] - k[1], V], F32) for k in TB_LOADS}
         vec_rows = sb("vec_rows", [P, P * PACK], F32)
         ident = sb("ident", [P, P], F32)
         bounds = sb("bounds", [P, PACK, PASSES], F32)
         neg_factors = sb("neg_factors", [P, PACK, PASSES], F32)
-        table_warm = sb("table_warm", [P, 2], F32)
         gap_first = sb("gap_first", [P, PACK, J], F32)
         vec_bank = psum.tile([P, PACK, P], F32, name="vec_bank")
         w_raw = sb("w_raw", [P, PASSES, R], I32)
         w_codes = sb("w_codes", [P, PASSES, PACK, P], I32)
-        ws_raw = sb("ws_raw", [P, PASSES, R], U8)
-        w_plane = sb("w_plane", [P, PASSES, PACK, P], U8)
+        w_scale_raw = sb("w_scale_raw", [P, PASSES, R], U8)
+        w_scale = sb("w_scale", [P, PASSES, PACK, P], U8)
         wb_codes = sb("wb_codes", [P, 2 * N], U8)
-        wb_plane = sb("wb_plane", [P, N], U8)
+        wb_scale = sb("wb_scale", [P, N], U8)
         rs_sb = sb("rs_sb", [P, HALVES, N], F32)
         rs_scaled = sb("rs_scaled", [P, HALVES, N], F32)
         picked_t = sb("picked_t", [P, PACK, J], F32)
         u_bf = [sb("u_bf_%d" % z, [P, J, PACK], BF16) for z in range(PASSES)]
         u_codes = {1: sb("u_codes_1", [P, J], U32)}
-        u_plane = [sb("u_plane_%d" % z, [P, J], U8) for z in range(PASSES)]
+        u_scale = [sb("u_scale_%d" % z, [P, J], U8) for z in range(PASSES)]
         a_bank = [psum.tile([P, PACK, HALF], F32, name="a_bank_%d" % h) for h in range(HALVES)]
         p_bank = [psum.tile([P, N], F32, name="p_bank_%d" % h) for h in range(HALVES)]
+        picked_b = {}
 
-        def gather(engine, dst, window, offsets):
-            if engine == "scalar":
-                nc.scalar.activation(dst, window.indirect(offsets), ACT.Copy)
-            else:
-                nc.vector.tensor_copy(dst, window.indirect(offsets))
+        def load(tiles, rows, z, first):
+            key = [k for k in tiles if k[:2] == (z, first)][0]
+            nc.sync.dma_start(tiles[key][:], rows[z, :, key[1] : key[2], :])
 
-        def window(tiles, z, t):
+        def plane(tiles, z, t):
             key = [k for k in tiles if k[0] == z and k[1] <= t < k[2]][0]
             return tiles[key][:, t - key[1], :]
 
-        def load(tiles, rows, z, t):
-            key = [k for k in tiles if k[:2] == (z, t)][0]
-            nc.sync.dma_start(tiles[key][:], rows[z, :, key[1] : key[2], :])
-
-        def bound(z, t):
-            return bounds[:, t, z : z + 1]
-
-        def neg_factor(z, t):
-            return neg_factors[:, t, z : z + 1]
-
-        def load_w_scale(q):
-            nc.sync.dma_start(
-                ws_raw[32 * q : 32 * q + 4, :, :].bitcast(I32),
-                w_scales[:, 4 * q : 4 * q + 4, :].rearrange("z r c -> r z c").bitcast(I32),
-            )
-
-        def load_wb_scale(q):
-            nc.sync.dma_start(
-                wb_plane[32 * q : 32 * q + 4, :].bitcast(I32), wb_scales[0, 4 * q : 4 * q + 4, :].bitcast(I32)
-            )
-
-        picked_b = {}
+        def gather(on_vector, dst, window, entries, lo, hi):
+            picked = window.indirect(entries[:, lo // PER_COL : hi // PER_COL])
+            if on_vector:
+                nc.vector.tensor_copy(dst[:, lo:hi], picked)
+            else:
+                nc.scalar.activation(dst[:, lo:hi], picked, ACT.Copy)
 
         def pick_b(z, t):
             picked_b[z, t] = sb("picked_b_%d_%d" % (z, t), [P, J], F32)
-            gather("vector" if t == 1 else "scalar", picked_b[z, t][:], window(xb_sb, z, t), list_b[:])
+            gather(t == XB_PLANE_ON_VECTOR, picked_b[z, t], plane(xb_sb, z, t), list_b, 0, J)
+
+        def pick_t(t, lo, hi):
+            gather(t == TB_PLANE_ON_VECTOR, picked_t[:, t, :], plane(tb_sb, 0, t), list_t, lo, hi)
 
         def make_gap(z, t, gap, parts):
             picked_a = sb("picked_a_%d_%d" % (z, t), [P, J], F32)
             for lo, hi in parts:
-                gather("scalar", picked_a[:, lo:hi], window(xa_sb, z, t), list_a[:, lo // PER_COL : hi // PER_COL])
+                gather(False, picked_a, plane(xa_sb, z, t), list_a, lo, hi)
             for lo, hi in parts:
                 nc.vector.scalar_tensor_tensor(
-                    gap[:, lo:hi], picked_b[z, t][:, lo:hi], bound(z, t), picked_a[:, lo:hi], ALU.min, ALU.subtract
+                    gap[:, lo:hi],
+                    picked_b[z, t][:, lo:hi],
+                    bounds[:, t, z : z + 1],
+                    picked_a[:, lo:hi],
+                    ALU.min,
+                    ALU.subtract,
                 )
 
         def make_u(z, t, parts):
             gap = sb("gap_%d_%d" % (z, t), [P, J], F32)
             make_gap(z, t, gap, parts)
             for lo, hi in parts:
-                nc.vector.tensor_scalar(u_bf[z][:, lo:hi, t], gap[:, lo:hi], neg_factor(z, t), None, ALU.mult)
+                nc.vector.tensor_scalar(
+                    u_bf[z][:, lo:hi, t], gap[:, lo:hi], neg_factors[:, t, z : z + 1], None, ALU.mult
+                )
 
         def quantize_u(z, lo, hi):
             nc.vector.quantize_mx(
                 out=u_codes[z][:, lo:hi].bitcast(E5M2X4),
-                scales=u_plane[z][:, lo:hi],
+                scales=u_scale[z][:, lo:hi],
                 in_=u_bf[z][:, lo:hi, :].rearrange("p j t -> p (j t)"),
             )
 
@@ -136,39 +137,36 @@ def tile_list_boundedgaps_overtable_rowpeaks_kernel(
                 nc.tensor.matmul_mx(
                     out=a_bank[h][:, t, :],
                     lhsT=w_codes[:, z, t, :].bitcast(E5M2X4),
-                    lhsT_scale=w_plane[:, z, t, :],
+                    lhsT_scale=w_scale[:, z, t, :],
                     rhs=u_codes[z][:, cols].bitcast(E5M2X4),
-                    rhs_scale=u_plane[z][:, cols],
+                    rhs_scale=u_scale[z][:, cols],
                     start=(z == 0 and t == 0),
                     stop=(z == PASSES - 1 and t == PACK - 1),
                 )
 
-        def pick_t(t, lo, hi):
-            gather(
-                "vector" if t == PACK - 1 else "scalar",
-                picked_t[:, t, lo:hi], tb_sb[t // 2][:, t % 2, :], list_t[:, lo // PER_COL : hi // PER_COL],
+        def deal_columns(dst, src):
+            nc.vector.tensor_copy(
+                dst[:].rearrange("p z t m -> p z m t"), src[:].rearrange("p z (m t) -> p z m t", t=PACK)
             )
 
-        halves = [(h * HALF, (h + 1) * HALF) for h in range(HALVES)]
-
-        whole = [(0, J)]
-        nc.vector.memset(table_warm[:, 0:1], 0.0)
-        nc.scalar.activation(table_warm[:, 1:2], table_warm[:, 0:1], ACT.Copy)
         nc.vector.memset(vec_rows[:], 0.0)
-        nc.vector.memset(ws_raw[:].rearrange("p z c -> p (z c)").bitcast(U32), 0)
+        nc.vector.memset(w_scale_raw[:].rearrange("p z c -> p (z c)").bitcast(U32), 0)
         make_identity(nc, ident[:])
-        nc.gpsimd.memset(wb_plane[:].bitcast(U32), 0)
+        nc.gpsimd.memset(wb_scale[:].bitcast(U32), 0)
 
         load(xb_sb, xb_rows, 0, 0)
         nc.sync.dma_start(list_b[:], offs2)
-        nc.sync.dma_start(vec_rows[4:12:4, :], hb.rearrange("(z c) o -> z (c o)", z=PASSES))
-        nc.sync.dma_start(vec_rows[12:20:4, :], fk.rearrange("(z c) o -> z (c o)", z=PASSES))
+        nc.sync.dma_start(vec_rows[HB_ROWS, :], hb.rearrange("(z c) o -> z (c o)", z=PASSES))
+        nc.sync.dma_start(vec_rows[FK_ROWS, :], fk.rearrange("(z c) o -> z (c o)", z=PASSES))
         load(xa_sb, xa_rows, 0, 0)
         nc.sync.dma_start(list_a[:], offs)
         load(xa_sb, xa_rows, 0, 1)
         load(xb_sb, xb_rows, 0, 2)
         for q in range(QUADS):
-            load_w_scale(q)
+            nc.sync.dma_start(
+                w_scale_raw[32 * q : 32 * q + 4, :, :].bitcast(I32),
+                w_scales[:, 4 * q : 4 * q + 4, :].rearrange("z r c -> r z c").bitcast(I32),
+            )
         load(xa_sb, xa_rows, 0, 2)
         nc.sync.dma_start(w_raw[:], w_words.rearrange("z p c r -> p z (c r)").bitcast(I32))
         load(xb_sb, xb_rows, 1, 0)
@@ -177,91 +175,89 @@ def tile_list_boundedgaps_overtable_rowpeaks_kernel(
             load(xa_sb, xa_rows, 1, t)
         load(xb_sb, xb_rows, 1, PACK - 1)
         load(xa_sb, xa_rows, 1, PACK - 1)
-        for e in range(2):
-            nc.sync.dma_start(tb_sb[e][:], tb_rows[:, 2 * e : 2 * e + 2, :])
+        for z, first, end in TB_LOADS:
+            load(tb_sb, tb_rows, z, first)
         nc.sync.dma_start(wb_codes[:], wb_words[0])
         for q in range(QUADS):
-            load_wb_scale(q)
+            nc.sync.dma_start(
+                wb_scale[32 * q : 32 * q + 4, :].bitcast(I32), wb_scales[0, 4 * q : 4 * q + 4, :].bitcast(I32)
+            )
         nc.sync.dma_start(rs_sb[:], rs.rearrange("(h p) n -> p h n", p=P))
 
         for t in range(PACK):
-            nc.tensor.transpose(vec_bank[:, t, :], vec_rows[:, t :: PACK], ident[:])
-        nc.vector.tensor_copy(bounds[:], vec_bank[:, :, 4:12:4])
-        nc.vector.tensor_scalar(neg_factors[:], vec_bank[:, :, 12:20:4], -1.0, None, ALU.mult)
+            nc.tensor.transpose(vec_bank[:, t, :], vec_rows[:, t::PACK], ident[:])
+        nc.vector.tensor_copy(bounds[:], vec_bank[:, :, HB_ROWS])
+        nc.vector.tensor_scalar(neg_factors[:], vec_bank[:, :, FK_ROWS], -1.0, None, ALU.mult)
 
-        for e in range(2):
-            for t in (2 * e, 2 * e + 1):
-                pick_b(0, t)
-            for t in (2 * e, 2 * e + 1):
-                make_gap(0, t, gap_first[:, t, :], whole)
-        nc.vector.tensor_copy(
-            w_plane[:].rearrange("p z t m -> p z m t"), ws_raw[:].rearrange("p z (m t) -> p z m t", t=PACK)
-        )
+        for z, first, end in XB_LOADS[:2]:
+            for t in range(first, end):
+                pick_b(z, t)
+            for t in range(first, end):
+                make_gap(z, t, gap_first[:, t, :], WHOLE)
+        deal_columns(w_scale, w_scale_raw)
         nc.vector.tensor_tensor(
-            u_bf[0][:].rearrange("p (c i) t -> p c t i", i=4),
-            gap_first[:].rearrange("p t (c i) -> p c t i", i=4),
-            neg_factors[:, :, 0:1].unsqueeze(1).to_broadcast([P, J // 4, PACK, 4]),
+            u_bf[0][:].rearrange("p (c i) t -> p c t i", i=RUN),
+            gap_first[:].rearrange("p t (c i) -> p c t i", i=RUN),
+            neg_factors[:, :, 0:1].unsqueeze(1).to_broadcast([P, J // RUN, PACK, RUN]),
             ALU.mult,
         )
-        nc.vector.tensor_copy(
-            w_codes[:].rearrange("p z t m -> p z m t"), w_raw[:].rearrange("p z (m t) -> p z m t", t=PACK)
-        )
+        deal_columns(w_codes, w_raw)
+
         for t in range(PACK - 1):
             pick_b(1, t)
-        make_u(1, 0, whole)
-        make_u(1, 1, whole)
+        make_u(1, 0, WHOLE)
+        make_u(1, 1, WHOLE)
         u_codes[0] = sb("u_codes_0", [P, J], U32, tag="gap_1_1")
         quantize_u(0, 0, J)
         for h in range(HALVES):
             first_product(0, h)
-        make_u(1, 2, whole)
+        make_u(1, 2, WHOLE)
         pick_b(1, 3)
-        make_u(1, 3, halves)
-        for h in range(HALVES):
-            quantize_u(1, h * HALF, (h + 1) * HALF)
+        make_u(1, 3, IN_HALVES)
+        for h, (lo, hi) in enumerate(IN_HALVES):
+            quantize_u(1, lo, hi)
             first_product(1, h)
-        for t in (0, 1):
+
+        for t in range(*TB_LOADS[0][1:]):
             pick_t(t, 0, J)
-        for lo, hi in halves:
-            for t in (2, 3):
+        for lo, hi in IN_HALVES:
+            for t in range(*TB_LOADS[1][1:]):
                 pick_t(t, lo, hi)
         nc.scalar.activation(rs_scaled[:], rs_sb[:], ACT.Copy, scale=0.3)
 
         over = [sb("over_%d" % h, [P, HALF, PACK], BF16) for h in range(HALVES)]
         hid = [sb("hid_%d" % h, [P, HALF * PACK], BF16) for h in range(HALVES)]
         hid_codes = [sb("hid_codes_%d" % h, [P, HALF], U32) for h in range(HALVES)]
-        hid_plane = [sb("hid_plane_%d" % h, [P, HALF], U8) for h in range(HALVES)]
+        hid_scale = [sb("hid_scale_%d" % h, [P, HALF], U8) for h in range(HALVES)]
         size = [sb("size_%d" % h, [P, N], F32) for h in range(HALVES)]
         shifted = [sb("shifted_%d" % h, [P, N], F32) for h in range(HALVES)]
         divisor = [sb("divisor_%d" % h, [P, 1], F32) for h in range(HALVES)]
         inverse = [sb("inverse_%d" % h, [P, 1], F32) for h in range(HALVES)]
         result = [sb("result_%d" % h, [P, N], F32) for h in range(HALVES)]
 
-        for h in range(HALVES):
+        for h, (lo, hi) in enumerate(IN_HALVES):
             nc.vector.tensor_tensor(
-                over[h][:].rearrange("p (c i) t -> p c t i", i=4),
-                a_bank[h][:].rearrange("p t (c i) -> p c t i", i=4),
-                picked_t[:, :, h * HALF : (h + 1) * HALF].rearrange("p t (c i) -> p c t i", i=4),
+                over[h][:].rearrange("p (c i) t -> p c t i", i=RUN),
+                a_bank[h][:].rearrange("p t (c i) -> p c t i", i=RUN),
+                picked_t[:, :, lo:hi].rearrange("p t (c i) -> p c t i", i=RUN),
                 ALU.subtract,
             )
             nc.vector.tensor_scalar(hid[h][:], over[h][:].rearrange("p j t -> p (j t)"), 0.0, None, ALU.max)
-            nc.vector.quantize_mx(out=hid_codes[h][:].bitcast(E5M2X4), scales=hid_plane[h][:], in_=hid[h][:])
+            nc.vector.quantize_mx(out=hid_codes[h][:].bitcast(E5M2X4), scales=hid_scale[h][:], in_=hid[h][:])
             nc.tensor.matmul_mx(
                 out=p_bank[h][:],
                 lhsT=hid_codes[h][:].bitcast(E5M2X4),
-                lhsT_scale=hid_plane[h][:],
+                lhsT_scale=hid_scale[h][:],
                 rhs=wb_codes[:].bitcast(E2M1X4),
-                rhs_scale=wb_plane[:],
+                rhs_scale=wb_scale[:],
                 start=True,
                 stop=True,
             )
             nc.scalar.activation(size[h][:], p_bank[h][:], ACT.Abs)
-        for h in range(HALVES):
-            nc.vector.tensor_scalar(
-                shifted[h][:], size[h][:], 0.2, None, ALU.add, ALU.max, accum_out=divisor[h][:]
-            )
+        for h, (lo, hi) in enumerate(IN_HALVES):
+            nc.vector.tensor_scalar(shifted[h][:], size[h][:], 0.2, None, ALU.add, ALU.max, accum_out=divisor[h][:])
             nc.vector.reciprocal(inverse[h][:], divisor[h][:])
             nc.vector.scalar_tensor_tensor(
                 result[h][:], p_bank[h][:], inverse[h][:], rs_scaled[:, h, :], ALU.mult, ALU.add
             )
-            nc.sync.dma_start(out[h * HALF : (h + 1) * HALF, :], result[h][:])
+            nc.sync.dma_start(out[lo:hi, :], result[h][:])

from contextlib import ExitStack

import concourse.mybir as mybir
from concourse.masks import make_identity

K, T, J, S, R, V, N = 1024, 1024, 256, 512, 512, 512, 256
FLOPS = 2 * K * R * J + 2 * J * R * N

F32 = mybir.dt.float32
BF16 = mybir.dt.bfloat16
I32 = mybir.dt.int32
U32 = mybir.dt.uint32
U16 = mybir.dt.uint16
U8 = mybir.dt.uint8
E5M2X4 = mybir.dt.float8_e5m2_x4
E2M1X4 = mybir.dt.float4_e2m1fn_x4
ALU = mybir.AluOpType
ACT = mybir.ActivationFunctionType

P = 128
PACK = 4
PASSES = K // (P * PACK)
HALF = 128
HALVES = J // HALF
PER_COL = 16
QUADS = 4
RUN = 4
WHOLE = [(0, J)]
IN_HALVES = [(h * HALF, (h + 1) * HALF) for h in range(HALVES)]

XA_LOADS = [(0, 0, 1), (0, 1, 2), (0, 2, 4), (1, 0, 1), (1, 1, 2), (1, 2, 3), (1, 3, 4)]
XB_LOADS = [(0, 0, 2), (0, 2, 4), (1, 0, 3), (1, 3, 4)]
TB_LOADS = [(0, 0, 2), (0, 2, 4)]
XB_PLANE_ON_VECTOR = 1
TB_PLANE_ON_VECTOR = PACK - 1
HB_ROWS = slice(4, 12, 4)
FK_ROWS = slice(12, 20, 4)


def tile_list_boundedgaps_overtable_rowpeaks_kernel(
    tc, xa, xb, hb, fk, w_words, w_scales, tb, wb_words, wb_scales, rs, offs, offs2, offs3, out
):
    nc = tc.nc
    xa_rows = xa.rearrange("(z p t) c -> z p t c", z=PASSES, t=PACK)
    xb_rows = xb.rearrange("(z p t) c -> z p t c", z=PASSES, t=PACK)
    tb_rows = tb.rearrange("(z p t) c -> z p t c", z=1, t=PACK)

    with ExitStack() as ctx:
        keep = ctx.enter_context(tc.tile_pool(name="keep", bufs=1))
        psum = ctx.enter_context(tc.psum_pool(name="psum", bufs=1))

        def sb(name, shape, dtype, tag=None):
            return keep.tile(shape, dtype, name=name, tag=tag or name, align_bytes=64)

        list_a = sb("list_a", [P, J // PER_COL], U16)
        list_b = sb("list_b", [P, J // PER_COL], U16)
        list_t = sb("list_t", [P, J // PER_COL], U16)
        xa_sb = {k: sb("xa_%d_%d" % k[:2], [P, k[2] - k[1], T], F32) for k in XA_LOADS}
        xb_sb = {k: sb("xb_%d_%d" % k[:2], [P, k[2] - k[1], S], F32) for k in XB_LOADS}
        tb_sb = {k: sb("tb_%d_%d" % k[:2], [P, k[2] - k[1], V], F32) for k in TB_LOADS}
        vec_rows = sb("vec_rows", [P, P * PACK], F32)
        ident = sb("ident", [P, P], F32)
        bounds = sb("bounds", [P, PACK, PASSES], F32)
        neg_factors = sb("neg_factors", [P, PACK, PASSES], F32)
        gap_first = sb("gap_first", [P, PACK, J], F32)
        vec_bank = psum.tile([P, PACK, P], F32, name="vec_bank")
        w_raw = sb("w_raw", [P, PASSES, R], I32)
        w_codes = sb("w_codes", [P, PASSES, PACK, P], I32)
        w_scale_raw = sb("w_scale_raw", [P, PASSES, R], U8)
        w_scale = sb("w_scale", [P, PASSES, PACK, P], U8)
        wb_codes = sb("wb_codes", [P, 2 * N], U8)
        wb_scale = sb("wb_scale", [P, N], U8)
        rs_sb = sb("rs_sb", [P, HALVES, N], F32)
        rs_scaled = sb("rs_scaled", [P, HALVES, N], F32)
        picked_t = sb("picked_t", [P, PACK, J], F32)
        u_bf = [sb("u_bf_%d" % z, [P, J, PACK], BF16) for z in range(PASSES)]
        u_codes = {1: sb("u_codes_1", [P, J], U32)}
        u_scale = [sb("u_scale_%d" % z, [P, J], U8) for z in range(PASSES)]
        a_bank = [psum.tile([P, PACK, HALF], F32, name="a_bank_%d" % h) for h in range(HALVES)]
        p_bank = [psum.tile([P, N], F32, name="p_bank_%d" % h) for h in range(HALVES)]
        picked_b = {}

        def load(tiles, rows, z, first):
            key = [k for k in tiles if k[:2] == (z, first)][0]
            nc.sync.dma_start(tiles[key][:], rows[z, :, key[1] : key[2], :])

        def plane(tiles, z, t):
            key = [k for k in tiles if k[0] == z and k[1] <= t < k[2]][0]
            return tiles[key][:, t - key[1], :]

        def gather(on_vector, dst, window, entries, lo, hi):
            picked = window.indirect(entries[:, lo // PER_COL : hi // PER_COL])
            if on_vector:
                nc.vector.tensor_copy(dst[:, lo:hi], picked)
            else:
                nc.scalar.activation(dst[:, lo:hi], picked, ACT.Copy)

        def pick_b(z, t):
            picked_b[z, t] = sb("picked_b_%d_%d" % (z, t), [P, J], F32)
            gather(t == XB_PLANE_ON_VECTOR, picked_b[z, t], plane(xb_sb, z, t), list_b, 0, J)

        def pick_t(t, lo, hi):
            gather(t == TB_PLANE_ON_VECTOR, picked_t[:, t, :], plane(tb_sb, 0, t), list_t, lo, hi)

        def make_gap(z, t, gap, parts):
            picked_a = sb("picked_a_%d_%d" % (z, t), [P, J], F32)
            for lo, hi in parts:
                gather(False, picked_a, plane(xa_sb, z, t), list_a, lo, hi)
            for lo, hi in parts:
                nc.vector.scalar_tensor_tensor(
                    gap[:, lo:hi],
                    picked_b[z, t][:, lo:hi],
                    bounds[:, t, z : z + 1],
                    picked_a[:, lo:hi],
                    ALU.min,
                    ALU.subtract,
                )

        def make_u(z, t, parts):
            gap = sb("gap_%d_%d" % (z, t), [P, J], F32)
            make_gap(z, t, gap, parts)
            for lo, hi in parts:
                nc.vector.tensor_scalar(
                    u_bf[z][:, lo:hi, t], gap[:, lo:hi], neg_factors[:, t, z : z + 1], None, ALU.mult
                )

        def quantize_u(z, lo, hi):
            nc.vector.quantize_mx(
                out=u_codes[z][:, lo:hi].bitcast(E5M2X4),
                scales=u_scale[z][:, lo:hi],
                in_=u_bf[z][:, lo:hi, :].rearrange("p j t -> p (j t)"),
            )

        def first_product(z, h):
            cols = slice(h * HALF, (h + 1) * HALF)
            for t in range(PACK):
                nc.tensor.matmul_mx(
                    out=a_bank[h][:, t, :],
                    lhsT=w_codes[:, z, t, :].bitcast(E5M2X4),
                    lhsT_scale=w_scale[:, z, t, :],
                    rhs=u_codes[z][:, cols].bitcast(E5M2X4),
                    rhs_scale=u_scale[z][:, cols],
                    start=(z == 0 and t == 0),
                    stop=(z == PASSES - 1 and t == PACK - 1),
                )

        def deal_columns(dst, src):
            nc.vector.tensor_copy(
                dst[:].rearrange("p z t m -> p z m t"), src[:].rearrange("p z (m t) -> p z m t", t=PACK)
            )

        nc.vector.memset(vec_rows[:], 0.0)
        nc.vector.memset(w_scale_raw[:].rearrange("p z c -> p (z c)").bitcast(U32), 0)
        make_identity(nc, ident[:])
        nc.gpsimd.memset(wb_scale[:].bitcast(U32), 0)

        load(xb_sb, xb_rows, 0, 0)
        nc.sync.dma_start(list_b[:], offs2)
        nc.sync.dma_start(vec_rows[HB_ROWS, :], hb.rearrange("(z c) o -> z (c o)", z=PASSES))
        nc.sync.dma_start(vec_rows[FK_ROWS, :], fk.rearrange("(z c) o -> z (c o)", z=PASSES))
        load(xa_sb, xa_rows, 0, 0)
        nc.sync.dma_start(list_a[:], offs)
        load(xa_sb, xa_rows, 0, 1)
        load(xb_sb, xb_rows, 0, 2)
        for q in range(QUADS):
            nc.sync.dma_start(
                w_scale_raw[32 * q : 32 * q + 4, :, :].bitcast(I32),
                w_scales[:, 4 * q : 4 * q + 4, :].rearrange("z r c -> r z c").bitcast(I32),
            )
        load(xa_sb, xa_rows, 0, 2)
        nc.sync.dma_start(w_raw[:], w_words.rearrange("z p c r -> p z (c r)").bitcast(I32))
        load(xb_sb, xb_rows, 1, 0)
        nc.sync.dma_start(list_t[:], offs3)
        for t in range(PACK - 1):
            load(xa_sb, xa_rows, 1, t)
        load(xb_sb, xb_rows, 1, PACK - 1)
        load(xa_sb, xa_rows, 1, PACK - 1)
        for z, first, end in TB_LOADS:
            load(tb_sb, tb_rows, z, first)
        nc.sync.dma_start(wb_codes[:], wb_words[0])
        for q in range(QUADS):
            nc.sync.dma_start(
                wb_scale[32 * q : 32 * q + 4, :].bitcast(I32), wb_scales[0, 4 * q : 4 * q + 4, :].bitcast(I32)
            )
        nc.sync.dma_start(rs_sb[:], rs.rearrange("(h p) n -> p h n", p=P))

        for t in range(PACK):
            nc.tensor.transpose(vec_bank[:, t, :], vec_rows[:, t::PACK], ident[:])
        nc.vector.tensor_copy(bounds[:], vec_bank[:, :, HB_ROWS])
        nc.vector.tensor_scalar(neg_factors[:], vec_bank[:, :, FK_ROWS], -1.0, None, ALU.mult)

        for z, first, end in XB_LOADS[:2]:
            for t in range(first, end):
                pick_b(z, t)
            for t in range(first, end):
                make_gap(z, t, gap_first[:, t, :], WHOLE)
        deal_columns(w_scale, w_scale_raw)
        nc.vector.tensor_tensor(
            u_bf[0][:].rearrange("p (c i) t -> p c t i", i=RUN),
            gap_first[:].rearrange("p t (c i) -> p c t i", i=RUN),
            neg_factors[:, :, 0:1].unsqueeze(1).to_broadcast([P, J // RUN, PACK, RUN]),
            ALU.mult,
        )
        deal_columns(w_codes, w_raw)

        for t in range(PACK - 1):
            pick_b(1, t)
        make_u(1, 0, WHOLE)
        make_u(1, 1, WHOLE)
        u_codes[0] = sb("u_codes_0", [P, J], U32, tag="gap_1_1")
        quantize_u(0, 0, J)
        for h in range(HALVES):
            first_product(0, h)
        make_u(1, 2, WHOLE)
        pick_b(1, 3)
        make_u(1, 3, IN_HALVES)
        for h, (lo, hi) in enumerate(IN_HALVES):
            quantize_u(1, lo, hi)
            first_product(1, h)

        for t in range(*TB_LOADS[0][1:]):
            pick_t(t, 0, J)
        for lo, hi in IN_HALVES:
            for t in range(*TB_LOADS[1][1:]):
                pick_t(t, lo, hi)
        nc.scalar.activation(rs_scaled[:], rs_sb[:], ACT.Copy, scale=0.3)

        over = [sb("over_%d" % h, [P, HALF, PACK], BF16) for h in range(HALVES)]
        hid = [sb("hid_%d" % h, [P, HALF * PACK], BF16) for h in range(HALVES)]
        hid_codes = [sb("hid_codes_%d" % h, [P, HALF], U32) for h in range(HALVES)]
        hid_scale = [sb("hid_scale_%d" % h, [P, HALF], U8) for h in range(HALVES)]
        size = [sb("size_%d" % h, [P, N], F32) for h in range(HALVES)]
        shifted = [sb("shifted_%d" % h, [P, N], F32) for h in range(HALVES)]
        divisor = [sb("divisor_%d" % h, [P, 1], F32) for h in range(HALVES)]
        inverse = [sb("inverse_%d" % h, [P, 1], F32) for h in range(HALVES)]
        result = [sb("result_%d" % h, [P, N], F32) for h in range(HALVES)]

        for h, (lo, hi) in enumerate(IN_HALVES):
            nc.vector.tensor_tensor(
                over[h][:].rearrange("p (c i) t -> p c t i", i=RUN),
                a_bank[h][:].rearrange("p t (c i) -> p c t i", i=RUN),
                picked_t[:, :, lo:hi].rearrange("p t (c i) -> p c t i", i=RUN),
                ALU.subtract,
            )
            nc.vector.tensor_scalar(hid[h][:], over[h][:].rearrange("p j t -> p (j t)"), 0.0, None, ALU.max)
            nc.vector.quantize_mx(out=hid_codes[h][:].bitcast(E5M2X4), scales=hid_scale[h][:], in_=hid[h][:])
            nc.tensor.matmul_mx(
                out=p_bank[h][:],
                lhsT=hid_codes[h][:].bitcast(E5M2X4),
                lhsT_scale=hid_scale[h][:],
                rhs=wb_codes[:].bitcast(E2M1X4),
                rhs_scale=wb_scale[:],
                start=True,
                stop=True,
            )
            nc.scalar.activation(size[h][:], p_bank[h][:], ACT.Abs)
        for h, (lo, hi) in enumerate(IN_HALVES):
            nc.vector.tensor_scalar(shifted[h][:], size[h][:], 0.2, None, ALU.add, ALU.max, accum_out=divisor[h][:])
            nc.vector.reciprocal(inverse[h][:], divisor[h][:])
            nc.vector.scalar_tensor_tensor(
                result[h][:], p_bank[h][:], inverse[h][:], rs_scaled[:, h, :], ALU.mult, ALU.add
            )
            nc.sync.dma_start(out[lo:hi, :], result[h][:])
